import numpy as np, ml_dtypes
CORES = [24,40,56,80,88,96]
N = 6
import mx_ref
NC, KT, ROOT = 128, 4, 5
BF = ml_dtypes.bfloat16
def setup_inputs(rng):
    def f(*shape):
        return mx_ref.flush((rng.standard_normal(shape, dtype=np.float32) * np.exp2(rng.integers(-2, 3, shape[:-1] + (1,)))).astype(BF))
    return {"w": f(N, 128, KT * 512), "x": f(N, 128, KT * 4 * NC)}
def setup_inputs_blocks(rng):
    d = setup_inputs(rng)
    for k in ("w", "x"): d[k] = mx_ref.spread(d[k], rng, 1)
    return d
def setup_inputs_wide(rng):
    d = setup_inputs(rng)
    for k in ("w", "x"): d[k] = mx_ref.flush((d[k].astype(np.float32) * np.exp2(rng.integers(-8, 9, (N, 1, 1))).astype(np.float32)).astype(BF))
    return d
def setup_inputs_zeros(rng):
    d = setup_inputs(rng); v = d["x"].reshape(N, 128, -1, 4).copy()
    v[np.broadcast_to((rng.random((N, 1, v.shape[2], 1)) < 0.33), v.shape)] = 0
    d["x"] = v.reshape(d["x"].shape)
    return d
def reference(w, x):
    QW = [mx_ref.quantize(w[ROOT][:, 512 * t:512 * t + 512]) for t in range(KT)]
    y = np.zeros((N, 128, NC), np.float32)
    for r in range(N):
        for t in range(KT):
            p = mx_ref.matmul(QW[t], mx_ref.quantize(x[r][:, 4 * NC * t:4 * NC * t + 4 * NC]))
            y[r] = p if t == 0 else y[r] + p
    return {"y": y}

@@ -1,0 +1,139 @@
+from concourse.bass import DstId, RemoteDMATransfer
+from concourse.mybir import dt
+
+KT, NC = 4, 128
+COLS = KT * NC
+HALF = COLS // 2
+ENG_CHIP = 16
+ENG_OUT = 8
+
+SCRATCH = {
+    "wb": ("sbuf", [128, 4 * COLS], "bfloat16"),
+    "xb": ("sbuf", [128, 4 * COLS], "bfloat16"),
+    "wq": ("sbuf", [128, COLS], "float8_e4m3fn_x4"),
+    "ws": ("sbuf", [128, COLS], "uint8"),
+    "xq": ("sbuf", [128, COLS], "float8_e4m3fn_x4"),
+    "xs": ("sbuf", [128, COLS], "uint8"),
+    "acc": ("psum", [128, 512], "float32"),
+    "yb": ("sbuf", [128, NC], "float32"),
+}
+SEMAPHORES = (["lw0", "lw1", "qw0", "qw1", "lx0", "lx1", "qx0", "qx1", "sent", "mm", "cp", "st"]
+              + ["p%d" % i for i in range(8)])
+
+SLICES = [(0, HALF), (HALF, COLS)]
+
+
+def _plan(T, topo):
+    cores = list(T.cores)
+    root = cores[T.root]
+    others = [c for c in cores if c != root]
+    near = [d for d in others if topo.may_write(root, d)]
+    far = [d for d in others if not topo.may_write(root, d)]
+    chip = [c for c in range(topo.CHIPS * topo.CORES_PER_CHIP) if topo.chip(c) == topo.chip(root) and c != root]
+    ports = [c for c in chip if all(topo.may_write(c, d) for d in far)]
+    here = [c for c in ports if topo.die(c) == topo.die(root)]
+    there = [c for c in ports if topo.die(c) != topo.die(root)]
+    pairs = [far[0:2], far[2:4]]
+    lead = [here[0], there[0]]
+    tail = [there[1], here[1]]
+    sends = [
+        (root, "c", 0, HALF, lead, ENG_CHIP),
+        (root, "s", 0, HALF, tail, ENG_CHIP),
+        (root, "c", HALF, COLS, tail, ENG_CHIP),
+        (root, "s", HALF, COLS, lead, ENG_CHIP),
+        (root, "s", 0, COLS, near, ENG_OUT),
+        (root, "c", 0, COLS, near, ENG_OUT),
+    ]
+    for i in range(2):
+        sends.append((lead[i], "c", 0, HALF, pairs[i], ENG_OUT))
+        sends.append((lead[i], "s", HALF, COLS, pairs[i], ENG_OUT))
+        sends.append((tail[i], "s", 0, HALF, pairs[i], ENG_OUT))
+        sends.append((tail[i], "c", HALF, COLS, pairs[i], ENG_OUT))
+    return root, sends
+
+
+def _view(T, kind, a, b):
+    return T.wq[:, a:b].bitcast(dt.uint8) if kind == "c" else T.ws[:, a:b]
+
+
+def _send(g, T, topo, src, kind, a, b, sem, dsts, n):
+    common = topo.mask(src, dsts[0])
+    for d in dsts[1:]:
+        common &= topo.mask(src, d)
+    bits = [e for e in range(common.bit_length()) if (common >> e) & 1][:n]
+    mask = sum(1 << e for e in bits)
+    ids = [DstId(rid=topo.addr(d)[0], pnc=topo.addr(d)[1]) for d in dsts]
+    g.remote_dma_fused([RemoteDMATransfer(dst_ids=ids, dma_engine_mask=mask, remote_sem=sem,
+                                          srcs=[_view(T, kind, a, b)], dsts=[_view(T, kind, a, b) for _ in dsts])],
+                       local_sem=T.sem.sent)
+    return len(bits)
+
+
+def rank_program(g, core, T, topo):
+    root, sends = _plan(T, topo)
+    rank = T.rank_of(core)
+    mine = [s for s in sends if s[0] == core]
+    if rank is None and not mine:
+        return
+    sem = T.sem
+    pieces = []
+    for s in sends:
+        if s[1:4] not in pieces:
+            pieces.append(s[1:4])
+    arrivals = [(s[1], s[2], s[3], sem["p%d" % pieces.index(s[1:4])], s[5]) for s in sends if core in s[4]]
+
+    if core == root:
+        for i, (a, b) in enumerate(SLICES):
+            g.sync.dma_start(T.wb[:, 4 * a:4 * b], T.w[:, 4 * a:4 * b]).then_inc(sem["lw%d" % i], 16)
+        for i, (a, b) in enumerate(SLICES):
+            g.vector.wait_ge(sem["lw%d" % i], 16)
+            g.vector.quantize_mx(T.wq[:, a:b], T.ws[:, a:b], T.wb[:, 4 * a:4 * b]).then_inc(sem["qw%d" % i], 1)
+    if rank is not None:
+        for i, (a, b) in enumerate(SLICES):
+            q = g.sync if (core == root or i == 0) else g.scalar
+            q.dma_start(T.xb[:, 4 * a:4 * b], T.x[:, 4 * a:4 * b]).then_inc(sem["lx%d" % i], 16)
+        for i, (a, b) in enumerate(SLICES):
+            g.vector.wait_ge(sem["lx%d" % i], 16)
+            g.vector.quantize_mx(T.xq[:, a:b], T.xs[:, a:b], T.xb[:, 4 * a:4 * b]).then_inc(sem["qx%d" % i], 1)
+
+    seen = set()
+    total = 0
+    for (_, kind, a, b, dsts, n) in mine:
+        if core == root:
+            for i, (sa, sb) in enumerate(SLICES):
+                if sa < b and a < sb and i not in seen:
+                    seen.add(i)
+                    g.wait_ge(sem["qw%d" % i], 1)
+        else:
+            for j, (k2, a2, b2, s2, n2) in enumerate(arrivals):
+                if k2 == kind and a2 < b and a < b2 and j not in seen:
+                    seen.add(j)
+                    g.wait_ge(s2, n2)
+        total += _send(g, T, topo, core, kind, a, b, sem["p%d" % pieces.index((kind, a, b))], dsts, n)
+    if mine:
+        g.wait_ge(sem.sent, total)
+    if rank is None:
+        return
+
+    got = set()
+    for t in range(KT):
+        a, b = t * NC, (t + 1) * NC
+        for i, (sa, sb) in enumerate(SLICES):
+            if sa < b and a < sb and ("x", i) not in got:
+                got.add(("x", i))
+                g.tensor.wait_ge(sem["qx%d" % i], 1)
+                if core == root:
+                    g.tensor.wait_ge(sem["qw%d" % i], 1)
+        for j, (k2, a2, b2, s2, n2) in enumerate(arrivals):
+            if a2 < b and a < b2 and j not in got:
+                got.add(j)
+                g.tensor.wait_ge(s2, n2)
+        mm = g.tensor.matmul_mx(T.acc[:, 0:NC], T.wq[:, a:b], T.ws[:, a:b], T.xq[:, a:b], T.xs[:, a:b],
+                                t == 0, t == KT - 1)
+    mm.then_inc(sem.mm, 1)
+
+    g.vector.wait_ge(sem.mm, 1)
+    g.vector.tensor_copy(T.yb[:], T.acc[:, 0:NC]).then_inc(sem.cp, 1)
+    g.sync.wait_ge(sem.cp, 1)
+    g.sync.dma_start(T.y[:], T.yb[:]).then_inc(sem.st, 16)
+    g.sync.wait_ge(sem.st, 16)

@@ -4,8 +4,6 @@ from concourse.mybir import dt
 KT, NC = 4, 128
 COLS = KT * NC
 HALF = COLS // 2
-ENG_CHIP = 16
-ENG_OUT = 8
 
 SCRATCH = {
     "wb": ("sbuf", [128, 4 * COLS], "bfloat16"),
@@ -17,10 +15,30 @@ SCRATCH = {
     "acc": ("psum", [128, 512], "float32"),
     "yb": ("sbuf", [128, NC], "float32"),
 }
-SEMAPHORES = (["lw0", "lw1", "qw0", "qw1", "lx0", "lx1", "qx0", "qx1", "sent", "mm", "cp", "st"]
-              + ["p%d" % i for i in range(8)])
+SEMAPHORES = (["lw%d" % i for i in range(KT)] + ["qw%d" % i for i in range(KT)]
+              + ["lx0", "lx1", "qx0", "qx1", "first", "sent", "mm", "cp", "st"] + ["p%d" % i for i in range(8)])
 
-SLICES = [(0, HALF), (HALF, COLS)]
+WSL = [(t * NC, (t + 1) * NC) for t in range(KT)]
+XSL = [(0, HALF), (HALF, COLS)]
+
+H = NC // 2
+STAGES = [
+    ("split", [("c", 0, H), ("c", H, NC)]),
+    ("each", [("s", 0, COLS), ("c", NC, 2 * NC)]),
+    ("split", [("c", 2 * NC, 3 * NC), ("c", 3 * NC, 4 * NC)]),
+]
+
+
+def _count(mask):
+    return sum((mask >> e) & 1 for e in range(mask.bit_length()))
+
+
+def _share(mode, pieces, k, group):
+    if mode == "split":
+        return [(pieces[k], group)]
+    if len(group) > 1:
+        return [(p, [group[k]]) for p in pieces]
+    return [(p, group) for p in pieces[k::2]]
 
 
 def _plan(T, topo):
@@ -31,86 +49,101 @@ def _plan(T, topo):
     far = [d for d in others if not topo.may_write(root, d)]
     chip = [c for c in range(topo.CHIPS * topo.CORES_PER_CHIP) if topo.chip(c) == topo.chip(root) and c != root]
     ports = [c for c in chip if all(topo.may_write(c, d) for d in far)]
+    rest = [c for c in chip if c not in ports]
     here = [c for c in ports if topo.die(c) == topo.die(root)]
     there = [c for c in ports if topo.die(c) != topo.die(root)]
-    pairs = [far[0:2], far[2:4]]
-    lead = [here[0], there[0]]
-    tail = [there[1], here[1]]
-    sends = [
-        (root, "c", 0, HALF, lead, ENG_CHIP),
-        (root, "s", 0, HALF, tail, ENG_CHIP),
-        (root, "c", HALF, COLS, tail, ENG_CHIP),
-        (root, "s", HALF, COLS, lead, ENG_CHIP),
-        (root, "s", 0, COLS, near, ENG_OUT),
-        (root, "c", 0, COLS, near, ENG_OUT),
-    ]
-    for i in range(2):
-        sends.append((lead[i], "c", 0, HALF, pairs[i], ENG_OUT))
-        sends.append((lead[i], "s", HALF, COLS, pairs[i], ENG_OUT))
-        sends.append((tail[i], "s", 0, HALF, pairs[i], ENG_OUT))
-        sends.append((tail[i], "c", HALF, COLS, pairs[i], ENG_OUT))
-    return root, sends
+    groups = [far[0:2], far[2:4], near]
+    relays = [[here[0], there[1]], [there[0], here[1]],
+              [[c for c in rest if topo.die(c) == topo.die(root)][0],
+               [c for c in rest if topo.die(c) != topo.die(root)][0]]]
+    on = _count(topo.mask(root, here[0]))
+    off = _count(topo.mask(here[0], far[0]))
+    calls = []
+    for j, (mode, pieces) in enumerate(STAGES):
+        takers = {p: [relays[i][k] for i in range(len(groups)) for k in range(2)
+                      if p in [q for (q, _) in _share(mode, pieces, k, groups[i])]] for p in pieces}
+        for keep in ([ports, rest] if j == 0 else [chip]):
+            calls.append((root, [p + ([c for c in takers[p] if c in keep], on // len(pieces)) for p in pieces]))
+    for i in range(len(groups)):
+        for k in range(2):
+            for (mode, pieces) in STAGES:
+                share = _share(mode, pieces, k, groups[i])
+                calls.append((relays[i][k], [p + (dsts, off // len(share)) for (p, dsts) in share]))
+    return root, calls
 
 
 def _view(T, kind, a, b):
     return T.wq[:, a:b].bitcast(dt.uint8) if kind == "c" else T.ws[:, a:b]
 
 
-def _send(g, T, topo, src, kind, a, b, sem, dsts, n):
-    common = topo.mask(src, dsts[0])
-    for d in dsts[1:]:
-        common &= topo.mask(src, d)
-    bits = [e for e in range(common.bit_length()) if (common >> e) & 1][:n]
-    mask = sum(1 << e for e in bits)
-    ids = [DstId(rid=topo.addr(d)[0], pnc=topo.addr(d)[1]) for d in dsts]
-    g.remote_dma_fused([RemoteDMATransfer(dst_ids=ids, dma_engine_mask=mask, remote_sem=sem,
-                                          srcs=[_view(T, kind, a, b)], dsts=[_view(T, kind, a, b) for _ in dsts])],
-                       local_sem=T.sem.sent)
-    return len(bits)
+def _issue(g, T, topo, src, transfers, sem_of, local_sem):
+    common = None
+    for (_, _, _, dsts, _) in transfers:
+        for d in dsts:
+            common = topo.mask(src, d) if common is None else common & topo.mask(src, d)
+    bits = [e for e in range(common.bit_length()) if (common >> e) & 1]
+    trs, used = [], 0
+    for (kind, a, b, dsts, n) in transfers:
+        mask = sum(1 << e for e in bits[used:used + n])
+        used += n
+        ids = [DstId(rid=topo.addr(d)[0], pnc=topo.addr(d)[1]) for d in dsts]
+        trs.append(RemoteDMATransfer(dst_ids=ids, dma_engine_mask=mask, remote_sem=sem_of[(kind, a, b)],
+                                     srcs=[_view(T, kind, a, b)], dsts=[_view(T, kind, a, b) for _ in dsts]))
+    g.remote_dma_fused(trs, local_sem=local_sem)
+    return used
 
 
 def rank_program(g, core, T, topo):
-    root, sends = _plan(T, topo)
+    root, calls = _plan(T, topo)
     rank = T.rank_of(core)
-    mine = [s for s in sends if s[0] == core]
+    mine = [trs for (src, trs) in calls if src == core]
     if rank is None and not mine:
         return
     sem = T.sem
-    pieces = []
-    for s in sends:
-        if s[1:4] not in pieces:
-            pieces.append(s[1:4])
-    arrivals = [(s[1], s[2], s[3], sem["p%d" % pieces.index(s[1:4])], s[5]) for s in sends if core in s[4]]
+    sem_of = {}
+    for (_, trs) in calls:
+        for tr in trs:
+            if tr[0:3] not in sem_of:
+                sem_of[tr[0:3]] = sem["p%d" % len(sem_of)]
+    arrivals = [(tr[0], tr[1], tr[2], sem_of[tr[0:3]], tr[4]) for (_, trs) in calls for tr in trs if core in tr[3]]
+    head = sum(tr[4] for tr in mine[0]) if mine else 0
 
     if core == root:
-        for i, (a, b) in enumerate(SLICES):
+        for i, (a, b) in enumerate(WSL):
             g.sync.dma_start(T.wb[:, 4 * a:4 * b], T.w[:, 4 * a:4 * b]).then_inc(sem["lw%d" % i], 16)
-        for i, (a, b) in enumerate(SLICES):
+        for i, (a, b) in enumerate(WSL):
             g.vector.wait_ge(sem["lw%d" % i], 16)
             g.vector.quantize_mx(T.wq[:, a:b], T.ws[:, a:b], T.wb[:, 4 * a:4 * b]).then_inc(sem["qw%d" % i], 1)
     if rank is not None:
-        for i, (a, b) in enumerate(SLICES):
-            q = g.sync if (core == root or i == 0) else g.scalar
+        for i, (a, b) in enumerate(XSL):
+            q = g.sync if i == 0 else g.scalar
+            if core == root:
+                q.wait_ge(sem.first, head)
             q.dma_start(T.xb[:, 4 * a:4 * b], T.x[:, 4 * a:4 * b]).then_inc(sem["lx%d" % i], 16)
-        for i, (a, b) in enumerate(SLICES):
+        for i, (a, b) in enumerate(XSL):
             g.vector.wait_ge(sem["lx%d" % i], 16)
             g.vector.quantize_mx(T.xq[:, a:b], T.xs[:, a:b], T.xb[:, 4 * a:4 * b]).then_inc(sem["qx%d" % i], 1)
 
     seen = set()
     total = 0
-    for (_, kind, a, b, dsts, n) in mine:
-        if core == root:
-            for i, (sa, sb) in enumerate(SLICES):
-                if sa < b and a < sb and i not in seen:
-                    seen.add(i)
-                    g.wait_ge(sem["qw%d" % i], 1)
+    for c, trs in enumerate(mine):
+        for (kind, a, b, _, _) in trs:
+            if core == root:
+                for i, (sa, sb) in enumerate(WSL):
+                    if sa < b and a < sb and i not in seen:
+                        seen.add(i)
+                        g.wait_ge(sem["qw%d" % i], 1)
+            else:
+                for j, (k2, a2, b2, s2, n2) in enumerate(arrivals):
+                    if k2 == kind and a2 < b and a < b2 and j not in seen:
+                        seen.add(j)
+                        g.wait_ge(s2, n2)
+        if c == 0:
+            _issue(g, T, topo, core, trs, sem_of, sem.first)
         else:
-            for j, (k2, a2, b2, s2, n2) in enumerate(arrivals):
-                if k2 == kind and a2 < b and a < b2 and j not in seen:
-                    seen.add(j)
-                    g.wait_ge(s2, n2)
-        total += _send(g, T, topo, core, kind, a, b, sem["p%d" % pieces.index((kind, a, b))], dsts, n)
+            total += _issue(g, T, topo, core, trs, sem_of, sem.sent)
     if mine:
+        g.wait_ge(sem.first, head)
         g.wait_ge(sem.sent, total)
     if rank is None:
         return
@@ -118,12 +151,12 @@ def rank_program(g, core, T, topo):
     got = set()
     for t in range(KT):
         a, b = t * NC, (t + 1) * NC
-        for i, (sa, sb) in enumerate(SLICES):
+        for i, (sa, sb) in enumerate(XSL):
             if sa < b and a < sb and ("x", i) not in got:
                 got.add(("x", i))
                 g.tensor.wait_ge(sem["qx%d" % i], 1)
-                if core == root:
-                    g.tensor.wait_ge(sem["qw%d" % i], 1)
+        if core == root:
+            g.tensor.wait_ge(sem["qw%d" % t], 1)
         for j, (k2, a2, b2, s2, n2) in enumerate(arrivals):
             if a2 < b and a < b2 and j not in got:
                 got.add(j)

from concourse.bass import DstId, RemoteDMATransfer
from concourse.mybir import dt

KT, NC = 4, 128
COLS = KT * NC
HALF = COLS // 2

SCRATCH = {
    "wb": ("sbuf", [128, 4 * COLS], "bfloat16"),
    "xb": ("sbuf", [128, 4 * COLS], "bfloat16"),
    "wq": ("sbuf", [128, COLS], "float8_e4m3fn_x4"),
    "ws": ("sbuf", [128, COLS], "uint8"),
    "xq": ("sbuf", [128, COLS], "float8_e4m3fn_x4"),
    "xs": ("sbuf", [128, COLS], "uint8"),
    "acc": ("psum", [128, 512], "float32"),
    "yb": ("sbuf", [128, NC], "float32"),
}
SEMAPHORES = (["lw%d" % i for i in range(KT)] + ["qw%d" % i for i in range(KT)]
              + ["lx0", "lx1", "qx0", "qx1", "first", "sent", "mm", "cp", "st"] + ["p%d" % i for i in range(8)])

WSL = [(t * NC, (t + 1) * NC) for t in range(KT)]
XSL = [(0, HALF), (HALF, COLS)]

H = NC // 2
STAGES = [
    ("split", [("c", 0, H), ("c", H, NC)]),
    ("each", [("s", 0, COLS), ("c", NC, 2 * NC)]),
    ("split", [("c", 2 * NC, 3 * NC), ("c", 3 * NC, 4 * NC)]),
]


def _count(mask):
    return sum((mask >> e) & 1 for e in range(mask.bit_length()))


def _share(mode, pieces, k, group):
    if mode == "split":
        return [(pieces[k], group)]
    if len(group) > 1:
        return [(p, [group[k]]) for p in pieces]
    return [(p, group) for p in pieces[k::2]]


def _plan(T, topo):
    cores = list(T.cores)
    root = cores[T.root]
    others = [c for c in cores if c != root]
    near = [d for d in others if topo.may_write(root, d)]
    far = [d for d in others if not topo.may_write(root, d)]
    chip = [c for c in range(topo.CHIPS * topo.CORES_PER_CHIP) if topo.chip(c) == topo.chip(root) and c != root]
    ports = [c for c in chip if all(topo.may_write(c, d) for d in far)]
    rest = [c for c in chip if c not in ports]
    here = [c for c in ports if topo.die(c) == topo.die(root)]
    there = [c for c in ports if topo.die(c) != topo.die(root)]
    groups = [far[0:2], far[2:4], near]
    relays = [[here[0], there[1]], [there[0], here[1]],
              [[c for c in rest if topo.die(c) == topo.die(root)][0],
               [c for c in rest if topo.die(c) != topo.die(root)][0]]]
    on = _count(topo.mask(root, here[0]))
    off = _count(topo.mask(here[0], far[0]))
    calls = []
    for j, (mode, pieces) in enumerate(STAGES):
        takers = {p: [relays[i][k] for i in range(len(groups)) for k in range(2)
                      if p in [q for (q, _) in _share(mode, pieces, k, groups[i])]] for p in pieces}
        for keep in ([ports, rest] if j == 0 else [chip]):
            calls.append((root, [p + ([c for c in takers[p] if c in keep], on // len(pieces)) for p in pieces]))
    for i in range(len(groups)):
        for k in range(2):
            for (mode, pieces) in STAGES:
                share = _share(mode, pieces, k, groups[i])
                calls.append((relays[i][k], [p + (dsts, off // len(share)) for (p, dsts) in share]))
    return root, calls


def _view(T, kind, a, b):
    return T.wq[:, a:b].bitcast(dt.uint8) if kind == "c" else T.ws[:, a:b]


def _issue(g, T, topo, src, transfers, sem_of, local_sem):
    common = None
    for (_, _, _, dsts, _) in transfers:
        for d in dsts:
            common = topo.mask(src, d) if common is None else common & topo.mask(src, d)
    bits = [e for e in range(common.bit_length()) if (common >> e) & 1]
    trs, used = [], 0
    for (kind, a, b, dsts, n) in transfers:
        mask = sum(1 << e for e in bits[used:used + n])
        used += n
        ids = [DstId(rid=topo.addr(d)[0], pnc=topo.addr(d)[1]) for d in dsts]
        trs.append(RemoteDMATransfer(dst_ids=ids, dma_engine_mask=mask, remote_sem=sem_of[(kind, a, b)],
                                     srcs=[_view(T, kind, a, b)], dsts=[_view(T, kind, a, b) for _ in dsts]))
    g.remote_dma_fused(trs, local_sem=local_sem)
    return used


def rank_program(g, core, T, topo):
    root, calls = _plan(T, topo)
    rank = T.rank_of(core)
    mine = [trs for (src, trs) in calls if src == core]
    if rank is None and not mine:
        return
    sem = T.sem
    sem_of = {}
    for (_, trs) in calls:
        for tr in trs:
            if tr[0:3] not in sem_of:
                sem_of[tr[0:3]] = sem["p%d" % len(sem_of)]
    arrivals = [(tr[0], tr[1], tr[2], sem_of[tr[0:3]], tr[4]) for (_, trs) in calls for tr in trs if core in tr[3]]
    head = sum(tr[4] for tr in mine[0]) if mine else 0

    if core == root:
        for i, (a, b) in enumerate(WSL):
            g.sync.dma_start(T.wb[:, 4 * a:4 * b], T.w[:, 4 * a:4 * b]).then_inc(sem["lw%d" % i], 16)
        for i, (a, b) in enumerate(WSL):
            g.vector.wait_ge(sem["lw%d" % i], 16)
            g.vector.quantize_mx(T.wq[:, a:b], T.ws[:, a:b], T.wb[:, 4 * a:4 * b]).then_inc(sem["qw%d" % i], 1)
    if rank is not None:
        for i, (a, b) in enumerate(XSL):
            q = g.sync if i == 0 else g.scalar
            if core == root:
                q.wait_ge(sem.first, head)
            q.dma_start(T.xb[:, 4 * a:4 * b], T.x[:, 4 * a:4 * b]).then_inc(sem["lx%d" % i], 16)
        for i, (a, b) in enumerate(XSL):
            g.vector.wait_ge(sem["lx%d" % i], 16)
            g.vector.quantize_mx(T.xq[:, a:b], T.xs[:, a:b], T.xb[:, 4 * a:4 * b]).then_inc(sem["qx%d" % i], 1)

    seen = set()
    total = 0
    for c, trs in enumerate(mine):
        for (kind, a, b, _, _) in trs:
            if core == root:
                for i, (sa, sb) in enumerate(WSL):
                    if sa < b and a < sb and i not in seen:
                        seen.add(i)
                        g.wait_ge(sem["qw%d" % i], 1)
            else:
                for j, (k2, a2, b2, s2, n2) in enumerate(arrivals):
                    if k2 == kind and a2 < b and a < b2 and j not in seen:
                        seen.add(j)
                        g.wait_ge(s2, n2)
        if c == 0:
            _issue(g, T, topo, core, trs, sem_of, sem.first)
        else:
            total += _issue(g, T, topo, core, trs, sem_of, sem.sent)
    if mine:
        g.wait_ge(sem.first, head)
        g.wait_ge(sem.sent, total)
    if rank is None:
        return

    got = set()
    for t in range(KT):
        a, b = t * NC, (t + 1) * NC
        for i, (sa, sb) in enumerate(XSL):
            if sa < b and a < sb and ("x", i) not in got:
                got.add(("x", i))
                g.tensor.wait_ge(sem["qx%d" % i], 1)
        if core == root:
            g.tensor.wait_ge(sem["qw%d" % t], 1)
        for j, (k2, a2, b2, s2, n2) in enumerate(arrivals):
            if a2 < b and a < b2 and j not in got:
                got.add(j)
                g.tensor.wait_ge(s2, n2)
        mm = g.tensor.matmul_mx(T.acc[:, 0:NC], T.wq[:, a:b], T.ws[:, a:b], T.xq[:, a:b], T.xs[:, a:b],
                                t == 0, t == KT - 1)
    mm.then_inc(sem.mm, 1)

    g.vector.wait_ge(sem.mm, 1)
    g.vector.tensor_copy(T.yb[:], T.acc[:, 0:NC]).then_inc(sem.cp, 1)
    g.sync.wait_ge(sem.cp, 1)
    g.sync.dma_start(T.y[:], T.yb[:]).then_inc(sem.st, 16)
    g.sync.wait_ge(sem.st, 16)
